import numpy as np
import ml_dtypes


def mxq(x, axis, fmt="e4m3"):
    dtype, down = {"e4m3": (ml_dtypes.float8_e4m3fn, 7), "e5m2": (ml_dtypes.float8_e5m2, 14)}[fmt]
    v = np.moveaxis(np.asarray(x, np.float32).astype(ml_dtypes.bfloat16).astype(np.float64), axis, -1)
    blocks = v.reshape(v.shape[:-1] + (-1, 32))
    amax = np.abs(blocks).max(-1, keepdims=True)
    byte = np.maximum(np.where(amax > 0, np.frexp(amax)[1] - 1 + 127, 0) - down, 1)
    scale = np.exp2(byte - 127.0)
    codes = (blocks / scale).astype(np.float32).astype(dtype).astype(np.float64)
    return np.moveaxis((codes * scale).reshape(v.shape), -1, axis)


WIDE = False


def mx_kscale(k):
    if not WIDE:
        return np.ones(k)
    levels = np.array([10, -10, 5, -5, 0])
    if k % 512:
        return np.exp2(np.random.permutation(np.resize(levels, k // 32))).repeat(32)
    a = np.empty((k // 512, 16))
    for p in range(k // 512):
        a[p, :8] = np.random.permutation(np.resize(levels, 8))
        for g in range(8):
            far = levels[np.abs(levels - a[p, g]) >= 10]
            a[p, g + 8] = far[np.random.randint(len(far))]
    return np.exp2(a.ravel()).repeat(32)


def f64(x):
    return np.asarray(x).astype(np.float64)


def striped(idx):
    return np.tile(idx.reshape(-1, 16).T, (8, 1)).astype(np.uint16)


def unstriped(offs):
    return offs[:16].T.reshape(-1).astype(np.int64)


def striped8(idx):
    return np.concatenate([x.reshape(-1, 16).T for x in idx]).astype(np.uint16)


def runs(offs, k):
    lists = np.stack([offs[16 * r : 16 * r + 16].T.reshape(-1) for r in range(8)]).astype(np.int64)
    return lists[np.arange(k) % 512 // 64]


def pack_weight(w):
    k, n = w.shape
    w = f64(np.asarray(w, np.float32).astype(ml_dtypes.bfloat16)).reshape(k // 32, 32, n)
    amax = np.abs(w).max(1)
    byte = np.clip(np.where(amax > 0, np.frexp(amax)[1] - 1 + 127 - 7, 1), 1, 254)
    scaled = (w * np.exp2(127.0 - byte)[:, None, :]).reshape(k, n).astype(np.float32)
    words = np.ascontiguousarray(scaled.reshape(k // 512, 128, 4, n).transpose(0, 1, 3, 2)).astype(ml_dtypes.float8_e4m3fn).view(np.uint8)
    return words, np.ascontiguousarray(byte.astype(np.uint8).reshape(k // 512, 16, n))


def unpack_weight(words, scales):
    g, p, n, _ = words.shape
    vals = np.ascontiguousarray(words).view(ml_dtypes.float8_e4m3fn).astype(np.float64) * np.repeat(np.exp2(scales.astype(np.float64) - 127.0), 8, axis=1)[..., None]
    return vals.transpose(0, 1, 3, 2).reshape(g * 512, n)


def relu(v):
    return np.maximum(v, 0.0)

def planes(y):
    n, m = y.shape
    v = y.astype(np.float32).astype(ml_dtypes.bfloat16).astype(np.float64).reshape(n // 32, 32, m)
    top = np.abs(v).max(1)
    byte = np.clip(np.where(top > 0, np.frexp(top)[1] - 1 + 127 - 7, 1), 1, 254)
    codes = (v * np.exp2(127.0 - byte)[:, None, :]).reshape(n, m).astype(np.float32).astype(ml_dtypes.float8_e4m3fn).view(np.uint8)
    words = codes.reshape(n // 512, 128, 4, m).transpose(0, 1, 3, 2)
    return np.ascontiguousarray(words), np.ascontiguousarray(byte.astype(np.uint8).reshape(n // 512, 16, m))


K, T, S, G, H, U, C = 512, 1024, 512, 2048, 512, 1024, 512


def setup_inputs():
    n = np.random.standard_normal
    s = mx_kscale(K)[:, None]
    packed_xT = pack_weight(n((K, T)) * s)
    packed_dT = pack_weight(n((K, G)) / s)
    return {
        "x_words": packed_xT[0],
        "x_scales": packed_xT[1],
        "d_words": packed_dT[0],
        "d_scales": packed_dT[1],
        "mem": n((H, U)).astype(np.float32),
        "gs": (np.random.uniform(0.5, 1.5, (K, 1)) / s).astype(np.float32),
        "offs": striped(np.random.permutation(T)[:S]),
        "k1": striped8(np.random.randint(0, G, (8, H))),
        "n1": striped8(np.stack([np.random.permutation(U)[:S] for _ in range(8)])),
        "n2": striped8(np.stack([np.random.permutation(U) for _ in range(8)])),
        "cand": striped(np.random.permutation(T)[:C]),
        "n3": striped8(np.stack([np.random.permutation(U) for _ in range(8)])),
    }


def reference(x_words, x_scales, d_words, d_scales, mem, gs, offs, k1, n1, n2, cand, n3):
    x_cand = unpack_weight(x_words, x_scales)[:, unstriped(cand)]
    d_k1 = unpack_weight(d_words, d_scales)[np.arange(K)[:, None], runs(k1, K)]
    xq = unpack_weight(x_words, x_scales)[:, unstriped(offs)]
    h = 0.0625 * (d_k1.T @ xq)
    pg = f64(mem).copy()
    pg[np.arange(H)[:, None], runs(n1, H)] = h
    z = f64(gs) * (pg - (0.5 * (pg[np.arange(H)[:, None], runs(n2, H)])))
    s = 0.0625 * ((x_cand.T @ mxq(z, 0, "e4m3")))
    rl = relu(s)
    ds = np.zeros((C, U))
    ds[np.arange(C)[:, None], runs(n3, C)] = rl
    out_0 = ds - (0.5 * s)
    return (out_0,) + planes(out_0)

@@ -1,0 +1,252 @@
+from contextlib import ExitStack
+
+import concourse.mybir as mybir
+from concourse.masks import make_identity
+
+K, T, S, G, H, U, C = 512, 1024, 512, 2048, 512, 1024, 512
+FLOPS = 2 * K * H * S + 2 * K * C * U
+
+F32 = mybir.dt.float32
+BF16 = mybir.dt.bfloat16
+I32 = mybir.dt.int32
+U32 = mybir.dt.uint32
+U16 = mybir.dt.uint16
+U8 = mybir.dt.uint8
+FP8X4 = mybir.dt.float8_e4m3fn_x4
+COPY = mybir.ActivationFunctionType.Copy
+RELU = mybir.ActivationFunctionType.Relu
+MULT = mybir.AluOpType.mult
+ADD = mybir.AluOpType.add
+
+P = 128
+PACK = 4
+HALF = 512
+CHUNK = 512
+LCOLS = HALF // 16
+
+
+def tile_picked_pqcpagemsend_none_po_kernel(tc, x_words, x_scales, d_words, d_scales, mem, gs, offs, k1, n1, n2, cand, n3, out_0, out_1, out_2):
+    nc = tc.nc
+    with ExitStack() as ctx:
+        lists = ctx.enter_context(tc.tile_pool(name="lists", bufs=1))
+        sb = ctx.enter_context(tc.tile_pool(name="sb", bufs=1))
+        ring = ctx.enter_context(tc.tile_pool(name="ring", bufs=3))
+        ps = ctx.enter_context(tc.psum_pool(name="ps", bufs=1))
+        ps2 = ctx.enter_context(tc.psum_pool(name="ps2", bufs=2))
+
+        def load_list(src, name):
+            tile = lists.tile(list(src.shape), U16, name=name)
+            nc.sync.dma_start(tile[:], src)
+            return tile
+
+        k1_t = load_list(k1, "k1_t")
+        d_sc = sb.tile([P, G], U8, name="d_sc")
+        nc.sync.dma_start(d_sc[:].bitcast(I32), d_scales[0].bitcast(I32).unsqueeze(1).broadcast_to([16, 8, G // 4]))
+        offs_t = load_list(offs, "offs_t")
+        x_w = sb.tile([P, T], I32, name="x_w")
+        nc.sync.dma_start(x_w[:], x_words[0].rearrange("p n t -> p (n t)").bitcast(I32))
+        x_sc = sb.tile([P, T], U8, name="x_sc")
+        for q in range(4):
+            rows = x_scales[0].bitcast(I32)[4 * q : 4 * q + 4, :]
+            nc.scalar.dma_start(x_sc[:].bitcast(I32)[32 * q : 32 * q + 32, :], rows.unsqueeze(0).broadcast_to([8, 4, T // 4]))
+        d_w = sb.tile([P, G], I32, name="d_w")
+        nc.sync.dma_start(d_w[:], d_words[0].rearrange("p n t -> p (n t)").bitcast(I32))
+        cand_t = load_list(cand, "cand_t")
+        n1_t = load_list(n1, "n1_t")
+        mem_rows = mem.rearrange("(p t) w -> t p w", t=PACK)
+        gs_t = sb.tile([P, PACK], F32, name="gs_t")
+        nc.sync.dma_start(gs_t[:], gs.rearrange("(p t) o -> p (t o)", t=PACK))
+        n2_t = load_list(n2, "n2_t")
+        n3_t = load_list(n3, "n3_t")
+        pg = []
+
+        def load_page(t):
+            tile = sb.tile([P, U], F32, name="pg%d" % t, tag="page%d" % t)
+            nc.sync.dma_start(tile[:], mem_rows[t])
+            pg.append(tile)
+
+        load_page(0)
+
+        ident = sb.tile([P, P], F32, name="ident")
+        make_identity(nc, ident[:])
+        d_plane = sb.tile([P, H], U8, name="d_plane", align_bytes=64)
+        nc.gpsimd.memset(d_plane[:], 0)
+
+        def deal(dst, src):
+            nc.vector.tensor_copy(dst.rearrange("p (t m) -> p t m", t=PACK), src.rearrange("p (m t) -> p t m", t=PACK))
+
+        dq_sc = sb.tile([P, H], U8, name="dq_sc", tag="page1")
+        nc.vector.tensor_copy(dq_sc[:], d_sc[:].indirect(k1_t[:]))
+        dd_sc = sb.tile([P, H], U8, name="dd_sc", tag="page3")
+        deal(dd_sc[:], dq_sc[:])
+        for j in range(4):
+            eng = nc.scalar if j % 2 == 0 else nc.sync
+            eng.dma_start(d_plane[:].bitcast(I32)[j:P:32, :], dd_sc[:].bitcast(I32)[8 * j : P : 32, :])
+        load_page(1)
+        xq_w = sb.tile([P, S], U32, name="xq_w", align_bytes=64)
+        nc.vector.tensor_copy(xq_w[:], x_w[:].bitcast(U32).indirect(offs_t[:]))
+        dq_w = sb.tile([P, H], U32, name="dq_w", tag="page2")
+        nc.vector.tensor_copy(dq_w[:], d_w[:].bitcast(U32).indirect(k1_t[:]))
+        xq_sc = sb.tile([P, S], U8, name="xq_sc", align_bytes=64)
+        nc.vector.tensor_copy(xq_sc[:], x_sc[:].indirect(offs_t[:]))
+        dd_w = sb.tile([P, H], U32, name="dd_w", align_bytes=64)
+        deal(dd_w[:].bitcast(I32), dq_w[:].bitcast(I32))
+
+        h = []
+        for t in range(PACK):
+            cols = slice(t * P, (t + 1) * P)
+            bank = ps2.tile([P, HALF], F32, name="mm")
+            nc.tensor.matmul_mx(out=bank[:], lhsT=dd_w[:, cols].bitcast(FP8X4), lhsT_scale=d_plane[:, cols], rhs=xq_w[:].bitcast(FP8X4), rhs_scale=xq_sc[:], start=True, stop=True)
+            h_t = sb.tile([P, S], F32, name="h%d" % t, tag="slot%d" % t)
+            nc.scalar.activation(h_t[:], bank[:], COPY, scale=0.0625)
+            h.append(h_t)
+
+        cq_sc = sb.tile([P, C], U8, name="cq_sc", tag="page2")
+        nc.vector.tensor_copy(cq_sc[:], x_sc[:].indirect(cand_t[:]))
+        cd_sc = sb.tile([P, C], U8, name="cd_sc", align_bytes=64)
+        deal(cd_sc[:], cq_sc[:])
+        load_page(2)
+        load_page(3)
+
+        a = [sb.tile([P, U], F32, name="a%d" % t) for t in range(PACK)]
+
+        def gather_half(dst, t, hf):
+            nc.vector.tensor_scalar(dst, a[t][:].indirect(n2_t[:, hf * LCOLS : (hf + 1) * LCOLS]), -0.5, 0.0, MULT, ADD)
+
+        def sum_half(banks, t, hf, g):
+            for b in range(4):
+                c0 = hf * HALF + b * P
+                nc.tensor.matmul(banks[b][:, t, :], a[t][:, c0 : c0 + P], ident[:], start=True, stop=False, is_transpose=True)
+            for b in range(4):
+                nc.tensor.matmul(banks[b][:, t, :], g[:, b * P : (b + 1) * P], ident[:], start=False, stop=True, is_transpose=True)
+
+        def finish_half(banks, hf):
+            zq = sb.tile([P, HALF * PACK], BF16, name="zq%d" % hf, align_bytes=64)
+            for pair in range(2):
+                back = ps2.tile([P, 2, 2, P], F32, name="back")
+                for i in range(2):
+                    z_t = ring.tile([P, 2, P, 2], BF16, name="z_t")
+                    nc.scalar.copy(z_t[:], banks[2 * pair + i][:].rearrange("w (u e) p -> w u p e", e=2))
+                    words = z_t[:].rearrange("w u p e -> w (u p e)").bitcast(F32)
+                    for u in range(2):
+                        nc.tensor.transpose(back[:, i, u, :], words[:, u * P : (u + 1) * P], ident[:])
+                dst = zq[:].bitcast(F32)[:, pair * 4 * P : (pair + 1) * 4 * P]
+                nc.scalar.copy(dst.rearrange("p (i w u) -> p i w u", i=2, u=2), back[:].rearrange("p i u w -> p i w u"))
+            return zq
+
+        def quantise_half(zq, hf):
+            z_w = sb.tile([P, HALF], U32, name="z_w%d" % hf, align_bytes=64)
+            z_sc = sb.tile([P, HALF], U8, name="z_sc%d" % hf, align_bytes=64)
+            nc.vector.quantize_mx(out=z_w[:].bitcast(FP8X4), scales=z_sc[:], in_=zq[:])
+            return z_w, z_sc
+
+        banks0 = [ps.tile([P, PACK, P], F32, name="zb0_%d" % b, tag="tb%d" % b) for b in range(4)]
+        for t in range(PACK):
+            nc.vector.tensor_copy(pg[t][:].indirect(n1_t[:]), h[t][:])
+            nc.scalar.activation(a[t][:], pg[t][:], COPY, scale=gs_t[:, t : t + 1])
+            if t >= 1:
+                g = sb.tile([P, HALF], F32, name="g0_%d" % (t - 1), tag="slot%d" % t)
+                gather_half(g[:], t - 1, 0)
+                sum_half(banks0, t - 1, 0, g)
+        g = sb.tile([P, HALF], F32, name="g0_3", tag="slot0")
+        gather_half(g[:], 3, 0)
+        sum_half(banks0, 3, 0, g)
+        g1 = sb.tile([P, PACK - 1, HALF], F32, name="g1", tag="page3")
+        cq_w = sb.tile([P, C], U32, name="cq_w", tag="slot0")
+        nc.vector.tensor_copy(cq_w[:], x_w[:].bitcast(U32).indirect(cand_t[:]))
+        for t in range(PACK - 1):
+            gather_half(g1[:, t, :], t, 1)
+        cd_w = sb.tile([P, C], U32, name="cd_w", align_bytes=64)
+        deal(cd_w[:].bitcast(I32), cq_w[:].bitcast(I32))
+        zq0 = finish_half(banks0, 0)
+        z = [quantise_half(zq0, 0)]
+        g1_last = sb.tile([P, HALF], F32, name="g1_last", tag="zq0", align_bytes=64)
+        gather_half(g1_last[:], PACK - 1, 1)
+
+        ds = {}
+        ms = [sb.tile([P, U], F32, name="ms%d" % t) for t in range(PACK - 1)]
+        out_rows = out_0.rearrange("(p t) w -> t p w", t=PACK)
+        o01 = sb.tile([P, 2, U], F32, name="o01")
+        o23 = [sb.tile([P, 2, CHUNK], F32, name="o23_%d" % c) for c in range(U // CHUNK)]
+        oq = [sb.tile([P, CHUNK, PACK], BF16, name="oq%d" % c, align_bytes=64) for c in range(U // CHUNK)]
+
+        def score(t, hf):
+            cols = slice(t * P, (t + 1) * P)
+            z_w, z_sc = z[hf]
+            bank = ps2.tile([P, HALF], F32, name="mm")
+            nc.tensor.matmul_mx(out=bank[:], lhsT=cd_w[:, cols].bitcast(FP8X4), lhsT_scale=cd_sc[:, cols], rhs=z_w[:].bitcast(FP8X4), rhs_scale=z_sc[:], start=True, stop=True)
+            rl = sb.tile([P, HALF], F32, name="rl%d_%d" % (t, hf), align_bytes=64)
+            nc.scalar.activation(rl[:], bank[:], RELU, scale=0.0625)
+            if hf == 0:
+                ds[t] = sb.tile([P, U], F32, name="ds%d" % t, tag={2: "zq1", 3: "rl2_1"}.get(t, "ds%d" % t), align_bytes=64)
+            nc.vector.tensor_copy(ds[t][:].indirect(n3_t[:, hf * LCOLS : (hf + 1) * LCOLS]), rl[:])
+            if t < PACK - 1:
+                nc.scalar.activation(ms[t][:, hf * HALF : (hf + 1) * HALF], bank[:], COPY, scale=-0.03125)
+            return bank
+
+        def combine(t):
+            for hf in range(2):
+                if t < 2:
+                    turned = ps.tile([P, 4, P], F32, name="turned", tag="tb%d" % (2 * t + hf))
+                else:
+                    turned = ps2.tile([P, 4, P], F32, name="turned", tag="back")
+                for i, src in enumerate((ms[t], ds[t])):
+                    for b in range(4):
+                        cols = slice(hf * HALF + b * P, hf * HALF + (b + 1) * P)
+                        nc.tensor.matmul(turned[:, b, :], src[:, cols], ident[:], start=(i == 0 and b == 0), stop=(i == 1 and b == 3), is_transpose=True)
+                turned_sb = sb.tile([P, 4, P], F32, name="turned_sb", tag="turned%d" % hf)
+                nc.scalar.copy(turned_sb[:], turned[:])
+                if t < 2:
+                    upright = ps2.tile([P, HALF], F32, name="upright", tag="back")
+                else:
+                    upright = ps.tile([P, HALF], F32, name="upright", tag="tb%d" % hf)
+                for b in range(4):
+                    nc.tensor.transpose(upright[:, b * P : (b + 1) * P], turned_sb[:, b, :], ident[:])
+                if t < 2:
+                    nc.scalar.copy(o01[:, t, hf * HALF : (hf + 1) * HALF], upright[:])
+                else:
+                    nc.scalar.copy(o23[hf][:, 0, :], upright[:])
+                    nc.scalar.dma_start(out_rows[t][:, hf * HALF : (hf + 1) * HALF], o23[hf][:, 0, :])
+            if t < 2:
+                nc.sync.dma_start(out_rows[t], o01[:, t, :])
+
+        score(0, 0)
+        score(1, 0)
+        banks1 = [ps.tile([P, PACK, P], F32, name="zb1_%d" % b, tag="tb%d" % b) for b in range(4)]
+        for t in range(PACK):
+            sum_half(banks1, t, 1, g1[:, t, :] if t < PACK - 1 else g1_last)
+        zq1 = finish_half(banks1, 1)
+        z.append(quantise_half(zq1, 1))
+        score(2, 0)
+        score(0, 1)
+        score(1, 1)
+        score(2, 1)
+        last = [score(3, 0), score(3, 1)]
+        combine(0)
+        combine(1)
+        for c in range(U // CHUNK):
+            nc.scalar.copy(oq[c][:, :, 0:2], o01[:, :, c * CHUNK : (c + 1) * CHUNK].rearrange("p e w -> p w e"))
+        combine(2)
+
+        factor = sb.tile([P, 1], F32, name="factor", tag="turned1")
+        nc.gpsimd.memset(factor[:], -0.03125)
+        o_w = sb.tile([P, U], I32, name="o_w", align_bytes=64)
+        o_sc = sb.tile([P, U], U8, name="o_sc", align_bytes=64)
+        words_out = out_1[0].rearrange("p n t -> p (n t)").bitcast(I32)
+        for c in range(U // CHUNK):
+            cols = slice(c * CHUNK, (c + 1) * CHUNK)
+            nc.vector.scalar_tensor_tensor(o23[c][:, 1, :], last[c][:], factor[:], ds[3][:, cols], MULT, ADD)
+            nc.sync.dma_start(out_rows[3][:, cols], o23[c][:, 1, :])
+        for c in range(U // CHUNK):
+            src = o23[c][:].rearrange("p e w -> p w e")
+            if c == 0:
+                nc.scalar.copy(oq[c][:, :, 2:4], src)
+            else:
+                nc.vector.tensor_copy(oq[c][:, :, 2:4], src)
+        for c in (1, 0):
+            cols = slice(c * CHUNK, (c + 1) * CHUNK)
+            nc.vector.quantize_mx(out=o_w[:, cols].bitcast(FP8X4), scales=o_sc[:, cols], in_=oq[c][:].rearrange("p w t -> p (w t)"))
+            nc.sync.dma_start(words_out[:, cols], o_w[:, cols])
+        for q in range(4):
+            eng = nc.scalar if q % 2 == 0 else nc.sync
+            eng.dma_start(out_2[0].bitcast(I32)[4 * q : 4 * q + 4, :], o_sc[:].bitcast(I32)[32 * q : 32 * q + 4, :])

@@ -21,7 +21,7 @@ ADD = mybir.AluOpType.add
 P = 128
 PACK = 4
 HALF = 512
-CHUNK = 512
+CHUNKS = [(0, 512), (512, 256), (768, 256)]
 LCOLS = HALF // 16
 
 
@@ -72,13 +72,13 @@ def tile_picked_pqcpagemsend_none_po_kernel(tc, x_words, x_scales, d_words, d_sc
         d_plane = sb.tile([P, H], U8, name="d_plane", align_bytes=64)
         nc.gpsimd.memset(d_plane[:], 0)
 
-        def deal(dst, src):
-            nc.vector.tensor_copy(dst.rearrange("p (t m) -> p t m", t=PACK), src.rearrange("p (m t) -> p t m", t=PACK))
+        def deal(dst, src, line):
+            nc.vector.tensor_copy(dst.rearrange("p (t c i) -> p c t i", t=PACK, i=line), src.rearrange("p (c i t) -> p c t i", t=PACK, i=line))
 
         dq_sc = sb.tile([P, H], U8, name="dq_sc", tag="page1")
         nc.vector.tensor_copy(dq_sc[:], d_sc[:].indirect(k1_t[:]))
         dd_sc = sb.tile([P, H], U8, name="dd_sc", tag="page3")
-        deal(dd_sc[:], dq_sc[:])
+        deal(dd_sc[:], dq_sc[:], 16)
         for j in range(4):
             eng = nc.scalar if j % 2 == 0 else nc.sync
             eng.dma_start(d_plane[:].bitcast(I32)[j:P:32, :], dd_sc[:].bitcast(I32)[8 * j : P : 32, :])
@@ -90,7 +90,7 @@ def tile_picked_pqcpagemsend_none_po_kernel(tc, x_words, x_scales, d_words, d_sc
         xq_sc = sb.tile([P, S], U8, name="xq_sc", align_bytes=64)
         nc.vector.tensor_copy(xq_sc[:], x_sc[:].indirect(offs_t[:]))
         dd_w = sb.tile([P, H], U32, name="dd_w", align_bytes=64)
-        deal(dd_w[:].bitcast(I32), dq_w[:].bitcast(I32))
+        deal(dd_w[:].bitcast(I32), dq_w[:].bitcast(I32), 4)
 
         h = []
         for t in range(PACK):
@@ -104,7 +104,7 @@ def tile_picked_pqcpagemsend_none_po_kernel(tc, x_words, x_scales, d_words, d_sc
         cq_sc = sb.tile([P, C], U8, name="cq_sc", tag="page2")
         nc.vector.tensor_copy(cq_sc[:], x_sc[:].indirect(cand_t[:]))
         cd_sc = sb.tile([P, C], U8, name="cd_sc", align_bytes=64)
-        deal(cd_sc[:], cq_sc[:])
+        deal(cd_sc[:], cq_sc[:], 16)
         load_page(2)
         load_page(3)
 
@@ -157,7 +157,7 @@ def tile_picked_pqcpagemsend_none_po_kernel(tc, x_words, x_scales, d_words, d_sc
         for t in range(PACK - 1):
             gather_half(g1[:, t, :], t, 1)
         cd_w = sb.tile([P, C], U32, name="cd_w", align_bytes=64)
-        deal(cd_w[:].bitcast(I32), cq_w[:].bitcast(I32))
+        deal(cd_w[:].bitcast(I32), cq_w[:].bitcast(I32), 4)
         zq0 = finish_half(banks0, 0)
         z = [quantise_half(zq0, 0)]
         g1_last = sb.tile([P, HALF], F32, name="g1_last", tag="zq0", align_bytes=64)
@@ -167,19 +167,19 @@ def tile_picked_pqcpagemsend_none_po_kernel(tc, x_words, x_scales, d_words, d_sc
         ms = [sb.tile([P, U], F32, name="ms%d" % t) for t in range(PACK - 1)]
         out_rows = out_0.rearrange("(p t) w -> t p w", t=PACK)
         o01 = sb.tile([P, 2, U], F32, name="o01")
-        o23 = [sb.tile([P, 2, CHUNK], F32, name="o23_%d" % c) for c in range(U // CHUNK)]
-        oq = [sb.tile([P, CHUNK, PACK], BF16, name="oq%d" % c, align_bytes=64) for c in range(U // CHUNK)]
+        o23 = [sb.tile([P, 2, n], F32, name="o23_%d" % c0) for c0, n in CHUNKS]
+        oq = [sb.tile([P, n, PACK], BF16, name="oq%d" % c0, align_bytes=64) for c0, n in CHUNKS]
 
-        def score(t, hf):
+        def score(t, hf, width=HALF):
             cols = slice(t * P, (t + 1) * P)
             z_w, z_sc = z[hf]
             bank = ps2.tile([P, HALF], F32, name="mm")
             nc.tensor.matmul_mx(out=bank[:], lhsT=cd_w[:, cols].bitcast(FP8X4), lhsT_scale=cd_sc[:, cols], rhs=z_w[:].bitcast(FP8X4), rhs_scale=z_sc[:], start=True, stop=True)
-            rl = sb.tile([P, HALF], F32, name="rl%d_%d" % (t, hf), align_bytes=64)
-            nc.scalar.activation(rl[:], bank[:], RELU, scale=0.0625)
+            rl = sb.tile([P, width], F32, name="rl%d_%d" % (t, hf), align_bytes=64)
+            nc.scalar.activation(rl[:], bank[:, 0:width], RELU, scale=0.0625)
             if hf == 0:
                 ds[t] = sb.tile([P, U], F32, name="ds%d" % t, tag={2: "zq1", 3: "rl2_1"}.get(t, "ds%d" % t), align_bytes=64)
-            nc.vector.tensor_copy(ds[t][:].indirect(n3_t[:, hf * LCOLS : (hf + 1) * LCOLS]), rl[:])
+            nc.vector.tensor_copy(ds[t][:].indirect(n3_t[:, hf * LCOLS : hf * LCOLS + width // 16]), rl[:])
             if t < PACK - 1:
                 nc.scalar.activation(ms[t][:, hf * HALF : (hf + 1) * HALF], bank[:], COPY, scale=-0.03125)
             return bank
@@ -205,8 +205,10 @@ def tile_picked_pqcpagemsend_none_po_kernel(tc, x_words, x_scales, d_words, d_sc
                 if t < 2:
                     nc.scalar.copy(o01[:, t, hf * HALF : (hf + 1) * HALF], upright[:])
                 else:
-                    nc.scalar.copy(o23[hf][:, 0, :], upright[:])
-                    nc.scalar.dma_start(out_rows[t][:, hf * HALF : (hf + 1) * HALF], o23[hf][:, 0, :])
+                    for c, (c0, n) in enumerate(CHUNKS):
+                        if c0 // HALF == hf:
+                            nc.scalar.copy(o23[c][:, 0, :], upright[:, c0 % HALF : c0 % HALF + n])
+                            nc.scalar.dma_start(out_rows[t][:, c0 : c0 + n], o23[c][:, 0, :])
             if t < 2:
                 nc.sync.dma_start(out_rows[t], o01[:, t, :])
 
@@ -217,15 +219,18 @@ def tile_picked_pqcpagemsend_none_po_kernel(tc, x_words, x_scales, d_words, d_sc
             sum_half(banks1, t, 1, g1[:, t, :] if t < PACK - 1 else g1_last)
         zq1 = finish_half(banks1, 1)
         z.append(quantise_half(zq1, 1))
-        score(2, 0)
+        score(2, 0, HALF // 2)
         score(0, 1)
         score(1, 1)
+        rl_rest = sb.tile([P, HALF // 2], F32, name="rl_rest", tag="rl0_1", align_bytes=64)
+        nc.scalar.activation(rl_rest[:], ms[2][:, HALF // 2 : HALF], RELU, scale=-2.0)
+        nc.vector.tensor_copy(ds[2][:].indirect(n3_t[:, LCOLS // 2 : LCOLS]), rl_rest[:])
         score(2, 1)
         last = [score(3, 0), score(3, 1)]
         combine(0)
         combine(1)
-        for c in range(U // CHUNK):
-            nc.scalar.copy(oq[c][:, :, 0:2], o01[:, :, c * CHUNK : (c + 1) * CHUNK].rearrange("p e w -> p w e"))
+        for c, (c0, n) in enumerate(CHUNKS):
+            nc.scalar.copy(oq[c][:, :, 0:2], o01[:, :, c0 : c0 + n].rearrange("p e w -> p w e"))
         combine(2)
 
         factor = sb.tile([P, 1], F32, name="factor", tag="turned1")
@@ -233,18 +238,18 @@ def tile_picked_pqcpagemsend_none_po_kernel(tc, x_words, x_scales, d_words, d_sc
         o_w = sb.tile([P, U], I32, name="o_w", align_bytes=64)
         o_sc = sb.tile([P, U], U8, name="o_sc", align_bytes=64)
         words_out = out_1[0].rearrange("p n t -> p (n t)").bitcast(I32)
-        for c in range(U // CHUNK):
-            cols = slice(c * CHUNK, (c + 1) * CHUNK)
-            nc.vector.scalar_tensor_tensor(o23[c][:, 1, :], last[c][:], factor[:], ds[3][:, cols], MULT, ADD)
+        for c, (c0, n) in enumerate(CHUNKS):
+            cols = slice(c0, c0 + n)
+            nc.vector.scalar_tensor_tensor(o23[c][:, 1, :], last[c0 // HALF][:, c0 % HALF : c0 % HALF + n], factor[:], ds[3][:, cols], MULT, ADD)
             nc.sync.dma_start(out_rows[3][:, cols], o23[c][:, 1, :])
-        for c in range(U // CHUNK):
+        for c in range(len(CHUNKS)):
             src = o23[c][:].rearrange("p e w -> p w e")
             if c == 0:
                 nc.scalar.copy(oq[c][:, :, 2:4], src)
             else:
                 nc.vector.tensor_copy(oq[c][:, :, 2:4], src)
-        for c in (1, 0):
-            cols = slice(c * CHUNK, (c + 1) * CHUNK)
+        for c in (1, 0, 2):
+            cols = slice(CHUNKS[c][0], CHUNKS[c][0] + CHUNKS[c][1])
             nc.vector.quantize_mx(out=o_w[:, cols].bitcast(FP8X4), scales=o_sc[:, cols], in_=oq[c][:].rearrange("p w t -> p (w t)"))
             nc.sync.dma_start(words_out[:, cols], o_w[:, cols])
         for q in range(4):

@@ -109,9 +109,12 @@ def tile_picked_pqcpagemsend_none_po_kernel(tc, x_words, x_scales, d_words, d_sc
         load_page(3)
 
         a = [sb.tile([P, U], F32, name="a%d" % t) for t in range(PACK)]
+        b_win = [sb.tile([P, U], F32, name="b%d" % t) for t in range(PACK)]
+        gs_half = sb.tile([P, PACK], F32, name="gs_half")
+        nc.scalar.activation(gs_half[:], gs_t[:], COPY, scale=-0.5)
 
         def gather_half(dst, t, hf):
-            nc.vector.tensor_scalar(dst, a[t][:].indirect(n2_t[:, hf * LCOLS : (hf + 1) * LCOLS]), -0.5, 0.0, MULT, ADD)
+            nc.vector.tensor_copy(dst, b_win[t][:].indirect(n2_t[:, hf * LCOLS : (hf + 1) * LCOLS]))
 
         def sum_half(banks, t, hf, g):
             for b in range(4):
@@ -143,7 +146,10 @@ def tile_picked_pqcpagemsend_none_po_kernel(tc, x_words, x_scales, d_words, d_sc
         banks0 = [ps.tile([P, PACK, P], F32, name="zb0_%d" % b, tag="tb%d" % b) for b in range(4)]
         for t in range(PACK):
             nc.vector.tensor_copy(pg[t][:].indirect(n1_t[:]), h[t][:])
-            nc.scalar.activation(a[t][:], pg[t][:], COPY, scale=gs_t[:, t : t + 1])
+            nc.scalar.activation(b_win[t][:], pg[t][:], COPY, scale=gs_half[:, t : t + 1])
+            for hf in range(2):
+                cols = slice(hf * HALF, (hf + 1) * HALF)
+                nc.scalar.activation(a[t][:, cols], b_win[t][:, cols], COPY, scale=-2.0)
             if t >= 1:
                 g = sb.tile([P, HALF], F32, name="g0_%d" % (t - 1), tag="slot%d" % t)
                 gather_half(g[:], t - 1, 0)

from contextlib import ExitStack

import concourse.mybir as mybir
from concourse.masks import make_identity

K, T, S, G, H, U, C = 512, 1024, 512, 2048, 512, 1024, 512
FLOPS = 2 * K * H * S + 2 * K * C * U

F32 = mybir.dt.float32
BF16 = mybir.dt.bfloat16
I32 = mybir.dt.int32
U32 = mybir.dt.uint32
U16 = mybir.dt.uint16
U8 = mybir.dt.uint8
FP8X4 = mybir.dt.float8_e4m3fn_x4
COPY = mybir.ActivationFunctionType.Copy
RELU = mybir.ActivationFunctionType.Relu
MULT = mybir.AluOpType.mult
ADD = mybir.AluOpType.add

P = 128
PACK = 4
HALF = 512
CHUNKS = [(0, 512), (512, 256), (768, 256)]
LCOLS = HALF // 16


def tile_picked_pqcpagemsend_none_po_kernel(tc, x_words, x_scales, d_words, d_scales, mem, gs, offs, k1, n1, n2, cand, n3, out_0, out_1, out_2):
    nc = tc.nc
    with ExitStack() as ctx:
        lists = ctx.enter_context(tc.tile_pool(name="lists", bufs=1))
        sb = ctx.enter_context(tc.tile_pool(name="sb", bufs=1))
        ring = ctx.enter_context(tc.tile_pool(name="ring", bufs=3))
        ps = ctx.enter_context(tc.psum_pool(name="ps", bufs=1))
        ps2 = ctx.enter_context(tc.psum_pool(name="ps2", bufs=2))

        def load_list(src, name):
            tile = lists.tile(list(src.shape), U16, name=name)
            nc.sync.dma_start(tile[:], src)
            return tile

        k1_t = load_list(k1, "k1_t")
        d_sc = sb.tile([P, G], U8, name="d_sc")
        nc.sync.dma_start(d_sc[:].bitcast(I32), d_scales[0].bitcast(I32).unsqueeze(1).broadcast_to([16, 8, G // 4]))
        offs_t = load_list(offs, "offs_t")
        x_w = sb.tile([P, T], I32, name="x_w")
        nc.sync.dma_start(x_w[:], x_words[0].rearrange("p n t -> p (n t)").bitcast(I32))
        x_sc = sb.tile([P, T], U8, name="x_sc")
        for q in range(4):
            rows = x_scales[0].bitcast(I32)[4 * q : 4 * q + 4, :]
            nc.scalar.dma_start(x_sc[:].bitcast(I32)[32 * q : 32 * q + 32, :], rows.unsqueeze(0).broadcast_to([8, 4, T // 4]))
        d_w = sb.tile([P, G], I32, name="d_w")
        nc.sync.dma_start(d_w[:], d_words[0].rearrange("p n t -> p (n t)").bitcast(I32))
        cand_t = load_list(cand, "cand_t")
        n1_t = load_list(n1, "n1_t")
        mem_rows = mem.rearrange("(p t) w -> t p w", t=PACK)
        gs_t = sb.tile([P, PACK], F32, name="gs_t")
        nc.sync.dma_start(gs_t[:], gs.rearrange("(p t) o -> p (t o)", t=PACK))
        n2_t = load_list(n2, "n2_t")
        n3_t = load_list(n3, "n3_t")
        pg = []

        def load_page(t):
            tile = sb.tile([P, U], F32, name="pg%d" % t, tag="page%d" % t)
            nc.sync.dma_start(tile[:], mem_rows[t])
            pg.append(tile)

        load_page(0)

        ident = sb.tile([P, P], F32, name="ident")
        make_identity(nc, ident[:])
        d_plane = sb.tile([P, H], U8, name="d_plane", align_bytes=64)
        nc.gpsimd.memset(d_plane[:], 0)

        def deal(dst, src, line):
            nc.vector.tensor_copy(dst.rearrange("p (t c i) -> p c t i", t=PACK, i=line), src.rearrange("p (c i t) -> p c t i", t=PACK, i=line))

        dq_sc = sb.tile([P, H], U8, name="dq_sc", tag="page1")
        nc.vector.tensor_copy(dq_sc[:], d_sc[:].indirect(k1_t[:]))
        dd_sc = sb.tile([P, H], U8, name="dd_sc", tag="page3")
        deal(dd_sc[:], dq_sc[:], 16)
        for j in range(4):
            eng = nc.scalar if j % 2 == 0 else nc.sync
            eng.dma_start(d_plane[:].bitcast(I32)[j:P:32, :], dd_sc[:].bitcast(I32)[8 * j : P : 32, :])
        load_page(1)
        xq_w = sb.tile([P, S], U32, name="xq_w", align_bytes=64)
        nc.vector.tensor_copy(xq_w[:], x_w[:].bitcast(U32).indirect(offs_t[:]))
        dq_w = sb.tile([P, H], U32, name="dq_w", tag="page2")
        nc.vector.tensor_copy(dq_w[:], d_w[:].bitcast(U32).indirect(k1_t[:]))
        xq_sc = sb.tile([P, S], U8, name="xq_sc", align_bytes=64)
        nc.vector.tensor_copy(xq_sc[:], x_sc[:].indirect(offs_t[:]))
        dd_w = sb.tile([P, H], U32, name="dd_w", align_bytes=64)
        deal(dd_w[:].bitcast(I32), dq_w[:].bitcast(I32), 4)

        h = []
        for t in range(PACK):
            cols = slice(t * P, (t + 1) * P)
            bank = ps2.tile([P, HALF], F32, name="mm")
            nc.tensor.matmul_mx(out=bank[:], lhsT=dd_w[:, cols].bitcast(FP8X4), lhsT_scale=d_plane[:, cols], rhs=xq_w[:].bitcast(FP8X4), rhs_scale=xq_sc[:], start=True, stop=True)
            h_t = sb.tile([P, S], F32, name="h%d" % t, tag="slot%d" % t)
            nc.scalar.activation(h_t[:], bank[:], COPY, scale=0.0625)
            h.append(h_t)

        cq_sc = sb.tile([P, C], U8, name="cq_sc", tag="page2")
        nc.vector.tensor_copy(cq_sc[:], x_sc[:].indirect(cand_t[:]))
        cd_sc = sb.tile([P, C], U8, name="cd_sc", align_bytes=64)
        deal(cd_sc[:], cq_sc[:], 16)
        load_page(2)
        load_page(3)

        a = [sb.tile([P, U], F32, name="a%d" % t) for t in range(PACK)]
        b_win = [sb.tile([P, U], F32, name="b%d" % t) for t in range(PACK)]
        gs_half = sb.tile([P, PACK], F32, name="gs_half")
        nc.scalar.activation(gs_half[:], gs_t[:], COPY, scale=-0.5)

        def gather_half(dst, t, hf):
            nc.vector.tensor_copy(dst, b_win[t][:].indirect(n2_t[:, hf * LCOLS : (hf + 1) * LCOLS]))

        def sum_half(banks, t, hf, g):
            for b in range(4):
                c0 = hf * HALF + b * P
                nc.tensor.matmul(banks[b][:, t, :], a[t][:, c0 : c0 + P], ident[:], start=True, stop=False, is_transpose=True)
            for b in range(4):
                nc.tensor.matmul(banks[b][:, t, :], g[:, b * P : (b + 1) * P], ident[:], start=False, stop=True, is_transpose=True)

        def finish_half(banks, hf):
            zq = sb.tile([P, HALF * PACK], BF16, name="zq%d" % hf, align_bytes=64)
            for pair in range(2):
                back = ps2.tile([P, 2, 2, P], F32, name="back")
                for i in range(2):
                    z_t = ring.tile([P, 2, P, 2], BF16, name="z_t")
                    nc.scalar.copy(z_t[:], banks[2 * pair + i][:].rearrange("w (u e) p -> w u p e", e=2))
                    words = z_t[:].rearrange("w u p e -> w (u p e)").bitcast(F32)
                    for u in range(2):
                        nc.tensor.transpose(back[:, i, u, :], words[:, u * P : (u + 1) * P], ident[:])
                dst = zq[:].bitcast(F32)[:, pair * 4 * P : (pair + 1) * 4 * P]
                nc.scalar.copy(dst.rearrange("p (i w u) -> p i w u", i=2, u=2), back[:].rearrange("p i u w -> p i w u"))
            return zq

        def quantise_half(zq, hf):
            z_w = sb.tile([P, HALF], U32, name="z_w%d" % hf, align_bytes=64)
            z_sc = sb.tile([P, HALF], U8, name="z_sc%d" % hf, align_bytes=64)
            nc.vector.quantize_mx(out=z_w[:].bitcast(FP8X4), scales=z_sc[:], in_=zq[:])
            return z_w, z_sc

        banks0 = [ps.tile([P, PACK, P], F32, name="zb0_%d" % b, tag="tb%d" % b) for b in range(4)]
        for t in range(PACK):
            nc.vector.tensor_copy(pg[t][:].indirect(n1_t[:]), h[t][:])
            nc.scalar.activation(b_win[t][:], pg[t][:], COPY, scale=gs_half[:, t : t + 1])
            for hf in range(2):
                cols = slice(hf * HALF, (hf + 1) * HALF)
                nc.scalar.activation(a[t][:, cols], b_win[t][:, cols], COPY, scale=-2.0)
            if t >= 1:
                g = sb.tile([P, HALF], F32, name="g0_%d" % (t - 1), tag="slot%d" % t)
                gather_half(g[:], t - 1, 0)
                sum_half(banks0, t - 1, 0, g)
        g = sb.tile([P, HALF], F32, name="g0_3", tag="slot0")
        gather_half(g[:], 3, 0)
        sum_half(banks0, 3, 0, g)
        g1 = sb.tile([P, PACK - 1, HALF], F32, name="g1", tag="page3")
        cq_w = sb.tile([P, C], U32, name="cq_w", tag="slot0")
        nc.vector.tensor_copy(cq_w[:], x_w[:].bitcast(U32).indirect(cand_t[:]))
        for t in range(PACK - 1):
            gather_half(g1[:, t, :], t, 1)
        cd_w = sb.tile([P, C], U32, name="cd_w", align_bytes=64)
        deal(cd_w[:].bitcast(I32), cq_w[:].bitcast(I32), 4)
        zq0 = finish_half(banks0, 0)
        z = [quantise_half(zq0, 0)]
        g1_last = sb.tile([P, HALF], F32, name="g1_last", tag="zq0", align_bytes=64)
        gather_half(g1_last[:], PACK - 1, 1)

        ds = {}
        ms = [sb.tile([P, U], F32, name="ms%d" % t) for t in range(PACK - 1)]
        out_rows = out_0.rearrange("(p t) w -> t p w", t=PACK)
        o01 = sb.tile([P, 2, U], F32, name="o01")
        o23 = [sb.tile([P, 2, n], F32, name="o23_%d" % c0) for c0, n in CHUNKS]
        oq = [sb.tile([P, n, PACK], BF16, name="oq%d" % c0, align_bytes=64) for c0, n in CHUNKS]

        def score(t, hf, width=HALF):
            cols = slice(t * P, (t + 1) * P)
            z_w, z_sc = z[hf]
            bank = ps2.tile([P, HALF], F32, name="mm")
            nc.tensor.matmul_mx(out=bank[:], lhsT=cd_w[:, cols].bitcast(FP8X4), lhsT_scale=cd_sc[:, cols], rhs=z_w[:].bitcast(FP8X4), rhs_scale=z_sc[:], start=True, stop=True)
            rl = sb.tile([P, width], F32, name="rl%d_%d" % (t, hf), align_bytes=64)
            nc.scalar.activation(rl[:], bank[:, 0:width], RELU, scale=0.0625)
            if hf == 0:
                ds[t] = sb.tile([P, U], F32, name="ds%d" % t, tag={2: "zq1", 3: "rl2_1"}.get(t, "ds%d" % t), align_bytes=64)
            nc.vector.tensor_copy(ds[t][:].indirect(n3_t[:, hf * LCOLS : hf * LCOLS + width // 16]), rl[:])
            if t < PACK - 1:
                nc.scalar.activation(ms[t][:, hf * HALF : (hf + 1) * HALF], bank[:], COPY, scale=-0.03125)
            return bank

        def combine(t):
            for hf in range(2):
                if t < 2:
                    turned = ps.tile([P, 4, P], F32, name="turned", tag="tb%d" % (2 * t + hf))
                else:
                    turned = ps2.tile([P, 4, P], F32, name="turned", tag="back")
                for i, src in enumerate((ms[t], ds[t])):
                    for b in range(4):
                        cols = slice(hf * HALF + b * P, hf * HALF + (b + 1) * P)
                        nc.tensor.matmul(turned[:, b, :], src[:, cols], ident[:], start=(i == 0 and b == 0), stop=(i == 1 and b == 3), is_transpose=True)
                turned_sb = sb.tile([P, 4, P], F32, name="turned_sb", tag="turned%d" % hf)
                nc.scalar.copy(turned_sb[:], turned[:])
                if t < 2:
                    upright = ps2.tile([P, HALF], F32, name="upright", tag="back")
                else:
                    upright = ps.tile([P, HALF], F32, name="upright", tag="tb%d" % hf)
                for b in range(4):
                    nc.tensor.transpose(upright[:, b * P : (b + 1) * P], turned_sb[:, b, :], ident[:])
                if t < 2:
                    nc.scalar.copy(o01[:, t, hf * HALF : (hf + 1) * HALF], upright[:])
                else:
                    for c, (c0, n) in enumerate(CHUNKS):
                        if c0 // HALF == hf:
                            nc.scalar.copy(o23[c][:, 0, :], upright[:, c0 % HALF : c0 % HALF + n])
                            nc.scalar.dma_start(out_rows[t][:, c0 : c0 + n], o23[c][:, 0, :])
            if t < 2:
                nc.sync.dma_start(out_rows[t], o01[:, t, :])

        score(0, 0)
        score(1, 0)
        banks1 = [ps.tile([P, PACK, P], F32, name="zb1_%d" % b, tag="tb%d" % b) for b in range(4)]
        for t in range(PACK):
            sum_half(banks1, t, 1, g1[:, t, :] if t < PACK - 1 else g1_last)
        zq1 = finish_half(banks1, 1)
        z.append(quantise_half(zq1, 1))
        score(2, 0, HALF // 2)
        score(0, 1)
        score(1, 1)
        rl_rest = sb.tile([P, HALF // 2], F32, name="rl_rest", tag="rl0_1", align_bytes=64)
        nc.scalar.activation(rl_rest[:], ms[2][:, HALF // 2 : HALF], RELU, scale=-2.0)
        nc.vector.tensor_copy(ds[2][:].indirect(n3_t[:, LCOLS // 2 : LCOLS]), rl_rest[:])
        score(2, 1)
        last = [score(3, 0), score(3, 1)]
        combine(0)
        combine(1)
        for c, (c0, n) in enumerate(CHUNKS):
            nc.scalar.copy(oq[c][:, :, 0:2], o01[:, :, c0 : c0 + n].rearrange("p e w -> p w e"))
        combine(2)

        factor = sb.tile([P, 1], F32, name="factor", tag="turned1")
        nc.gpsimd.memset(factor[:], -0.03125)
        o_w = sb.tile([P, U], I32, name="o_w", align_bytes=64)
        o_sc = sb.tile([P, U], U8, name="o_sc", align_bytes=64)
        words_out = out_1[0].rearrange("p n t -> p (n t)").bitcast(I32)
        for c, (c0, n) in enumerate(CHUNKS):
            cols = slice(c0, c0 + n)
            nc.vector.scalar_tensor_tensor(o23[c][:, 1, :], last[c0 // HALF][:, c0 % HALF : c0 % HALF + n], factor[:], ds[3][:, cols], MULT, ADD)
            nc.sync.dma_start(out_rows[3][:, cols], o23[c][:, 1, :])
        for c in range(len(CHUNKS)):
            src = o23[c][:].rearrange("p e w -> p w e")
            if c == 0:
                nc.scalar.copy(oq[c][:, :, 2:4], src)
            else:
                nc.vector.tensor_copy(oq[c][:, :, 2:4], src)
        for c in (1, 0, 2):
            cols = slice(CHUNKS[c][0], CHUNKS[c][0] + CHUNKS[c][1])
            nc.vector.quantize_mx(out=o_w[:, cols].bitcast(FP8X4), scales=o_sc[:, cols], in_=oq[c][:].rearrange("p w t -> p (w t)"))
            nc.sync.dma_start(words_out[:, cols], o_w[:, cols])
        for q in range(4):
            eng = nc.scalar if q % 2 == 0 else nc.sync
            eng.dma_start(out_2[0].bitcast(I32)[4 * q : 4 * q + 4, :], o_sc[:].bitcast(I32)[32 * q : 32 * q + 4, :])
